import numpy as np
import ml_dtypes

BF16 = ml_dtypes.bfloat16


def bf(x):
    return np.asarray(x, np.float32).astype(BF16)


def f32(x):
    return np.asarray(x, np.float32)


def f64(x):
    return np.asarray(x).astype(np.float64)


def striped(idx):
    return np.tile(idx.reshape(-1, 16).T, (8, 1))


S, K, M, N, E, Q, O = 256, 128, 128, 192, 2, 96, 512


def setup_inputs():
    return {"base": bf(np.random.standard_normal((M, S))), "x": bf(np.random.standard_normal((K, N))), "w": bf(1.2 * np.random.standard_normal((E, K, M)) / np.sqrt(K)), "w2": bf(np.random.standard_normal((M, O)) / np.sqrt(2 * M)), "b": f32(0.5 * np.random.standard_normal((O, 1))), "offs": striped(np.random.permutation(S)[:N])}


def reference(base, x, w, w2, b, offs):
    idx = offs[:16].T.reshape(-1)
    z = f64(base).copy()
    for e in range(E):
        z[:, idx[e * Q : (e + 1) * Q]] += f64(w)[e].T @ f64(x)[:, e * Q : (e + 1) * Q]
    y = f64(w2).T @ z
    return y + f64(b)

@@ -1,0 +1,57 @@
+import concourse.mybir as mybir
+from concourse.masks import make_identity
+
+P = 128
+TOKENS, ENTRIES, EXPERTS, FEATURES_OUT = 256, 192, 2, 512
+PIECE = ENTRIES // EXPERTS
+BLOCKS = FEATURES_OUT // P
+FLOPS = 2 * P * P * ENTRIES + 2 * P * FEATURES_OUT * TOKENS
+
+BF16, F32, U16 = mybir.dt.bfloat16, mybir.dt.float32, mybir.dt.uint16
+IDENTITY = mybir.ActivationFunctionType.Identity
+
+
+def tile_rows_thenproj_bias_kernel(tc, base, x, w, w2, b, offs, out):
+    nc = tc.nc
+    with (
+        tc.tile_pool(name="held", bufs=1) as held,
+        tc.psum_pool(name="psum", bufs=1) as psum,
+    ):
+        base_tile = held.tile([P, TOKENS], BF16, name="base_tile")
+        x_tile = held.tile([P, ENTRIES], BF16, name="x_tile")
+        w_tile = held.tile([P, EXPERTS, P], BF16, name="w_tile")
+        offsets = held.tile([P, ENTRIES // 16], U16, name="offsets")
+        w2_tile = held.tile([P, FEATURES_OUT], BF16, name="w2_tile")
+        bias = held.tile([P, BLOCKS], F32, name="bias")
+
+        nc.sync.dma_start(base_tile[:], base)
+        nc.sync.dma_start(offsets[:], offs)
+        nc.sync.dma_start(w_tile[:], w.rearrange("e k m -> k e m"))
+        nc.sync.dma_start(x_tile[:], x)
+        nc.sync.dma_start(w2_tile[:], w2)
+        nc.sync.dma_start(bias[:], b.rearrange("(a p) o -> p (a o)", p=P))
+
+        ident = held.tile([P, P], BF16, name="ident")
+        make_identity(nc, ident[:])
+
+        window = psum.tile([P, TOKENS], F32, name="window")
+        nc.tensor.matmul(window[:], ident[:], base_tile[:], start=True, stop=False)
+        for e in range(EXPERTS):
+            places = offsets[:, e * PIECE // 16 : (e + 1) * PIECE // 16]
+            entries = x_tile[:, e * PIECE : (e + 1) * PIECE]
+            nc.tensor.matmul(
+                window[:].indirect(places), w_tile[:, e, :], entries, start=False, stop=e == EXPERTS - 1
+            )
+
+        z = held.tile([P, TOKENS], BF16, name="z")
+        nc.vector.tensor_copy(z[:], window[:])
+
+        for a in range(BLOCKS):
+            y = psum.tile([P, TOKENS], F32, name=f"y{a}")
+            nc.tensor.matmul(y[:], w2_tile[:, a * P : (a + 1) * P], z[:], start=True, stop=True)
+            result = held.tile([P, TOKENS], F32, name=f"result{a}")
+            if a % 2 == 0:
+                nc.vector.tensor_scalar_add(result[:], y[:], bias[:, a : a + 1])
+            else:
+                nc.scalar.activation(result[:], y[:], IDENTITY, bias=bias[:, a : a + 1])
+            nc.sync.dma_start(out[a * P : (a + 1) * P, :], result[:])

@@ -5,6 +5,7 @@ P = 128
 TOKENS, ENTRIES, EXPERTS, FEATURES_OUT = 256, 192, 2, 512
 PIECE = ENTRIES // EXPERTS
 BLOCKS = FEATURES_OUT // P
+WARM_MATMULS, WARM_COLUMNS = 4, 512
 FLOPS = 2 * P * P * ENTRIES + 2 * P * FEATURES_OUT * TOKENS
 
 BF16, F32, U16 = mybir.dt.bfloat16, mybir.dt.float32, mybir.dt.uint16
@@ -24,12 +25,20 @@ def tile_rows_thenproj_bias_kernel(tc, base, x, w, w2, b, offs, out):
         w2_tile = held.tile([P, FEATURES_OUT], BF16, name="w2_tile")
         bias = held.tile([P, BLOCKS], F32, name="bias")
 
+        zeros = held.tile([P, WARM_COLUMNS], BF16, name="zeros")
+        nc.vector.memset(zeros[:], 0.0)
+        warm = psum.tile([P, WARM_COLUMNS], F32, name="warm")
+        for i in range(WARM_MATMULS):
+            nc.tensor.matmul(warm[:], zeros[:, :P], zeros[:], start=True, stop=True)
+        early = held.tile([P, 1], BF16, name="early")
+        nc.scalar.activation(early[:], zeros[:, 0:1], IDENTITY, bias=zeros[:, 0:1])
+
         nc.sync.dma_start(base_tile[:], base)
         nc.sync.dma_start(offsets[:], offs)
         nc.sync.dma_start(w_tile[:], w.rearrange("e k m -> k e m"))
         nc.sync.dma_start(x_tile[:], x)
         nc.sync.dma_start(w2_tile[:], w2)
-        nc.sync.dma_start(bias[:], b.rearrange("(a p) o -> p (a o)", p=P))
+        nc.sync.dma_start(bias[:], b.rearrange("(p a) o -> p (a o)", a=BLOCKS))
 
         ident = held.tile([P, P], BF16, name="ident")
         make_identity(nc, ident[:])
@@ -46,12 +55,13 @@ def tile_rows_thenproj_bias_kernel(tc, base, x, w, w2, b, offs, out):
         z = held.tile([P, TOKENS], BF16, name="z")
         nc.vector.tensor_copy(z[:], window[:])
 
+        out_blocks = out.rearrange("(p a) i -> p a i", a=BLOCKS)
         for a in range(BLOCKS):
             y = psum.tile([P, TOKENS], F32, name=f"y{a}")
-            nc.tensor.matmul(y[:], w2_tile[:, a * P : (a + 1) * P], z[:], start=True, stop=True)
+            nc.tensor.matmul(y[:], w2_tile[:, a::BLOCKS], z[:], start=True, stop=True)
             result = held.tile([P, TOKENS], F32, name=f"result{a}")
             if a % 2 == 0:
                 nc.vector.tensor_scalar_add(result[:], y[:], bias[:, a : a + 1])
             else:
                 nc.scalar.activation(result[:], y[:], IDENTITY, bias=bias[:, a : a + 1])
-            nc.sync.dma_start(out[a * P : (a + 1) * P, :], result[:])
+            nc.sync.dma_start(out_blocks[:, a, :], result[:])

@@ -5,7 +5,7 @@ P = 128
 TOKENS, ENTRIES, EXPERTS, FEATURES_OUT = 256, 192, 2, 512
 PIECE = ENTRIES // EXPERTS
 BLOCKS = FEATURES_OUT // P
-WARM_MATMULS, WARM_COLUMNS = 4, 512
+WARM_MATMULS, WARM_COLUMNS = 6, 256
 FLOPS = 2 * P * P * ENTRIES + 2 * P * FEATURES_OUT * TOKENS
 
 BF16, F32, U16 = mybir.dt.bfloat16, mybir.dt.float32, mybir.dt.uint16

@@ -4,6 +4,7 @@ from concourse.masks import make_identity
 P = 128
 TOKENS, ENTRIES, EXPERTS, FEATURES_OUT = 256, 192, 2, 512
 PIECE = ENTRIES // EXPERTS
+HALF = TOKENS // 2
 BLOCKS = FEATURES_OUT // P
 WARM_MATMULS, WARM_COLUMNS = 6, 256
 FLOPS = 2 * P * P * ENTRIES + 2 * P * FEATURES_OUT * TOKENS
@@ -17,6 +18,7 @@ def tile_rows_thenproj_bias_kernel(tc, base, x, w, w2, b, offs, out):
     with (
         tc.tile_pool(name="held", bufs=1) as held,
         tc.psum_pool(name="psum", bufs=1) as psum,
+        tc.psum_pool(name="y_pool", bufs=3) as y_pool,
     ):
         base_tile = held.tile([P, TOKENS], BF16, name="base_tile")
         x_tile = held.tile([P, ENTRIES], BF16, name="x_tile")
@@ -56,12 +58,13 @@ def tile_rows_thenproj_bias_kernel(tc, base, x, w, w2, b, offs, out):
         nc.vector.tensor_copy(z[:], window[:])
 
         out_blocks = out.rearrange("(p a) i -> p a i", a=BLOCKS)
+        left, right = slice(0, HALF), slice(HALF, TOKENS)
         for a in range(BLOCKS):
-            y = psum.tile([P, TOKENS], F32, name=f"y{a}")
-            nc.tensor.matmul(y[:], w2_tile[:, a::BLOCKS], z[:], start=True, stop=True)
+            y_left = y_pool.tile([P, HALF], F32, name="y_left")
+            y_right = y_pool.tile([P, HALF], F32, name="y_right")
+            nc.tensor.matmul(y_left[:], w2_tile[:, a::BLOCKS], z[:, left], start=True, stop=True)
+            nc.tensor.matmul(y_right[:], w2_tile[:, a::BLOCKS], z[:, right], start=True, stop=True)
             result = held.tile([P, TOKENS], F32, name=f"result{a}")
-            if a % 2 == 0:
-                nc.vector.tensor_scalar_add(result[:], y[:], bias[:, a : a + 1])
-            else:
-                nc.scalar.activation(result[:], y[:], IDENTITY, bias=bias[:, a : a + 1])
+            nc.vector.tensor_scalar_add(result[:, left], y_left[:], bias[:, a : a + 1])
+            nc.scalar.activation(result[:, right], y_right[:], IDENTITY, bias=bias[:, a : a + 1])
             nc.sync.dma_start(out_blocks[:, a, :], result[:])

import concourse.mybir as mybir
from concourse.masks import make_identity

P = 128
TOKENS, ENTRIES, EXPERTS, FEATURES_OUT = 256, 192, 2, 512
PIECE = ENTRIES // EXPERTS
HALF = TOKENS // 2
BLOCKS = FEATURES_OUT // P
WARM_MATMULS, WARM_COLUMNS = 6, 256
FLOPS = 2 * P * P * ENTRIES + 2 * P * FEATURES_OUT * TOKENS

BF16, F32, U16 = mybir.dt.bfloat16, mybir.dt.float32, mybir.dt.uint16
IDENTITY = mybir.ActivationFunctionType.Identity


def tile_rows_thenproj_bias_kernel(tc, base, x, w, w2, b, offs, out):
    nc = tc.nc
    with (
        tc.tile_pool(name="held", bufs=1) as held,
        tc.psum_pool(name="psum", bufs=1) as psum,
        tc.psum_pool(name="y_pool", bufs=3) as y_pool,
    ):
        base_tile = held.tile([P, TOKENS], BF16, name="base_tile")
        x_tile = held.tile([P, ENTRIES], BF16, name="x_tile")
        w_tile = held.tile([P, EXPERTS, P], BF16, name="w_tile")
        offsets = held.tile([P, ENTRIES // 16], U16, name="offsets")
        w2_tile = held.tile([P, FEATURES_OUT], BF16, name="w2_tile")
        bias = held.tile([P, BLOCKS], F32, name="bias")

        zeros = held.tile([P, WARM_COLUMNS], BF16, name="zeros")
        nc.vector.memset(zeros[:], 0.0)
        warm = psum.tile([P, WARM_COLUMNS], F32, name="warm")
        for i in range(WARM_MATMULS):
            nc.tensor.matmul(warm[:], zeros[:, :P], zeros[:], start=True, stop=True)
        early = held.tile([P, 1], BF16, name="early")
        nc.scalar.activation(early[:], zeros[:, 0:1], IDENTITY, bias=zeros[:, 0:1])

        nc.sync.dma_start(base_tile[:], base)
        nc.sync.dma_start(offsets[:], offs)
        nc.sync.dma_start(w_tile[:], w.rearrange("e k m -> k e m"))
        nc.sync.dma_start(x_tile[:], x)
        nc.sync.dma_start(w2_tile[:], w2)
        nc.sync.dma_start(bias[:], b.rearrange("(p a) o -> p (a o)", a=BLOCKS))

        ident = held.tile([P, P], BF16, name="ident")
        make_identity(nc, ident[:])

        window = psum.tile([P, TOKENS], F32, name="window")
        nc.tensor.matmul(window[:], ident[:], base_tile[:], start=True, stop=False)
        for e in range(EXPERTS):
            places = offsets[:, e * PIECE // 16 : (e + 1) * PIECE // 16]
            entries = x_tile[:, e * PIECE : (e + 1) * PIECE]
            nc.tensor.matmul(
                window[:].indirect(places), w_tile[:, e, :], entries, start=False, stop=e == EXPERTS - 1
            )

        z = held.tile([P, TOKENS], BF16, name="z")
        nc.vector.tensor_copy(z[:], window[:])

        out_blocks = out.rearrange("(p a) i -> p a i", a=BLOCKS)
        left, right = slice(0, HALF), slice(HALF, TOKENS)
        for a in range(BLOCKS):
            y_left = y_pool.tile([P, HALF], F32, name="y_left")
            y_right = y_pool.tile([P, HALF], F32, name="y_right")
            nc.tensor.matmul(y_left[:], w2_tile[:, a::BLOCKS], z[:, left], start=True, stop=True)
            nc.tensor.matmul(y_right[:], w2_tile[:, a::BLOCKS], z[:, right], start=True, stop=True)
            result = held.tile([P, TOKENS], F32, name=f"result{a}")
            nc.vector.tensor_scalar_add(result[:, left], y_left[:], bias[:, a : a + 1])
            nc.scalar.activation(result[:, right], y_right[:], IDENTITY, bias=bias[:, a : a + 1])
            nc.sync.dma_start(out_blocks[:, a, :], result[:])
